import numpy as np, ml_dtypes
CORES = [8,136,40,168]
N = 4
import mx_ref
BF = ml_dtypes.bfloat16
def entries(a):
    return np.ascontiguousarray(a.T).reshape(-1)
def table(e):
    return np.ascontiguousarray(np.reshape(e, (-1, 16)).T).astype(np.int32)
def cols(t, e):
    v = np.concatenate([t.reshape(128, -1, 4), np.zeros((128, 1, 4), BF)], axis=1)
    return np.ascontiguousarray(v[:, e]).reshape(128, -1)
def cut(t, i, w=512):
    return t[:, w * i:w * i + w]
def f(rng, *shape):
    return mx_ref.flush((rng.standard_normal(shape, dtype=np.float32) * np.exp2(rng.integers(-2, 3, shape[:-1] + (1,)))).astype(BF))
def wide(rng, *shape, cols=0):
    v = rng.standard_normal(shape, dtype=np.float32) * np.exp2(rng.integers(-12, 13, shape)).astype(np.float32)
    if cols: v *= np.repeat(np.exp2(rng.integers(-cols, cols + 1, shape[:-2] + (1, shape[-1] // 4))) * (rng.random(shape[:-2] + (1, shape[-1] // 4)) > 0.0625), 4, axis=-1).astype(np.float32)
    return mx_ref.flush(v.astype(BF))
C, R, CAPP = 128, 4, 32
def lists(rng, full=False, stay=False, fresh=False, one=False):
    sl = np.full((N, R, N, CAPP), -1); pa = rng.integers(0, C, (N, R, C))
    for t in range(R):
        if stay: continue
        for r in range(N):
            for d in range(N):
                if d == r: continue
                n = CAPP if full else rng.integers(0, CAPP + 1)
                sl[r, t, d, rng.permutation(CAPP)[:n]] = rng.integers(0, C, n)
        for d in range(N):
            far = C + np.flatnonzero(sl[:, t, d].reshape(-1) >= 0)
            pa[d, t, rng.permutation(C)[:far.size]] = far
            if full: continue
            if far.size: pa[d, t, rng.integers(0, C, C // 16)] = rng.choice(far, C // 16)
            pa[d, t, rng.permutation(C)[:C // 2 if fresh else C // 8]] = -1
    if fresh: pa[rng.integers(0, N), rng.integers(0, R)] = -1
    if one:
        o, j = rng.integers(0, N), rng.integers(0, C)
        for t in range(R - 1):
            q, c, k = (o + rng.integers(1, N)) % N, rng.integers(0, CAPP), rng.integers(0, C)
            sl[o, t, q, c] = j; pa[q, t, k] = C + o * CAPP + c
            o, j = q, k
        for q in range(N):
            c = rng.integers(0, CAPP)
            if q != o: sl[o, R - 1, q, c] = j
            pa[q, R - 1] = j if q == o else C + o * CAPP + c
    return {"sl": np.stack([table(sl[r]) for r in range(N)]), "pa": np.stack([table(pa[r]) for r in range(N)])}
def setup_inputs(rng):
    return {"x": f(rng, N, 128, 4 * C * (R + 1)), "w": f(rng, N, 128, 512 * (R + 1)), **lists(rng)}
def setup_inputs_stay(rng):
    return {**setup_inputs(rng), **lists(rng, stay=True)}
def setup_inputs_far(rng):
    return {**setup_inputs(rng), **lists(rng, full=True)}
def setup_inputs_one(rng):
    return {**setup_inputs(rng), **lists(rng, one=True)}
def setup_inputs_fresh(rng):
    return {**setup_inputs(rng), **lists(rng, fresh=True)}
def setup_inputs_spread(rng):
    d = setup_inputs(rng); d["x"] = wide(rng, N, 128, 4 * C * (R + 1), cols=8); return d
def check_inputs(d):
    b = []
    s = [entries(d["sl"][r]).reshape(R, N, CAPP) for r in range(N)]
    for r in range(N):
        p = entries(d["pa"][r]).reshape(R, C)
        if s[r].min() < -1 or s[r].max() >= C or (s[r][:, r] != -1).any(): b.append("sl")
        if p.min() < -1 or p.max() >= C + N * CAPP: b.append("pa"); continue
        for t in range(R):
            slots = np.concatenate([s[q][t, r] for q in range(N)])
            if (slots[p[t][p[t] >= C] - C] < 0).any(): b.append("pa"); break
    return b
def reference(x, w, sl, pa):
    s = [entries(sl[r]).reshape(R, N, CAPP) for r in range(N)]
    p = [entries(pa[r]).reshape(R, C) for r in range(N)]
    cache = [np.ascontiguousarray(cut(x[r], 0, 4 * C)) for r in range(N)]
    y = np.zeros((N, 128, C * (R + 1)), np.float32)
    for t in range(R + 1):
        if t > 0:
            after = []
            for r in range(N):
                slots = [cols(cache[q], s[q][t - 1, r]) for q in range(N)]
                every = np.concatenate([cache[r]] + slots + [cut(x[r], t, 4 * C)], axis=1)
                v = p[r][t - 1]
                after.append(cols(every, np.where(v < 0, C + N * CAPP + np.arange(C), v)))
            cache = after
        for r in range(N):
            y[r][:, C * t:C * t + C] = mx_ref.matmul(mx_ref.quantize(np.ascontiguousarray(cut(w[r], t))), mx_ref.quantize(cache[r]))
    return {"y": y}

@@ -1,0 +1,235 @@
+from concourse.bass import DstId, RemoteDMATransfer
+from concourse.mybir import dt, AluOpType, ActivationFunctionType
+
+CODE, PLANE = "float8_e4m3fn_x4", "uint8"
+N, C, R, CAPP = 4, 128, 4, 32
+SCRATCH = {
+    "xt": ("sbuf", [128, 2560], "bfloat16"), "wt": ("sbuf", [128, 2560], "bfloat16"),
+    "slw": ("sbuf", [128, 32], "int32"), "paw": ("sbuf", [128, 32], "int32"),
+    "base": ("sbuf", [128, 32], "int32"), "part": ("sbuf", [128, 32], "int32"), "low": ("sbuf", [128, 32], "int32"),
+    "fresh": ("sbuf", [128, 32], "int32"), "even": ("sbuf", [128, 24], "int32"), "odd": ("sbuf", [128, 24], "int32"),
+    "rep32": ("sbuf", [128, 24], "int32"), "rep": ("sbuf", [128, 24], "uint16"),
+    "neg": ("sbuf", [128, 32], "int32"), "add": ("sbuf", [128, 32], "int32"), "pav": ("sbuf", [128, 32], "int32"),
+    "paoff": ("sbuf", [128, 32], "uint16"), "sd": ("sbuf", [128, 64], "uint16"),
+    "k0c": ("sbuf", [128, 128], CODE), "k0p": ("sbuf", [128, 128], PLANE),
+    "k4c": ("sbuf", [128, 128], CODE), "k4p": ("sbuf", [128, 128], PLANE),
+    "wc": ("sbuf", [128, 640], CODE), "wp": ("sbuf", [128, 640], PLANE),
+    "ysb": ("sbuf", [128, 640], "float32"), "ps": ("psum", [128, 2560], "float32"),
+}
+for _t in range(1, 5):
+    SCRATCH["c%d" % _t] = ("sbuf", [128, 384], CODE)
+    SCRATCH["p%d" % _t] = ("sbuf", [128, 384], PLANE)
+for _t in range(4):
+    SCRATCH["sc%d" % _t] = ("sbuf", [128, 96], CODE)
+    SCRATCH["sp%d" % _t] = ("sbuf", [128, 96], PLANE)
+    SCRATCH["off%d" % _t] = ("sbuf", [128, 6], "uint16")
+for _t in range(1, 4):
+    SCRATCH["ga%d" % _t] = ("sbuf", [128, 128], "float32")
+    SCRATCH["lin%d" % _t] = ("sbuf", [128, 128], "float32")
+    SCRATCH["gb%d" % _t] = ("sbuf", [128, 256], "float32")
+    SCRATCH["tb%d" % _t] = ("sbuf", [128, 256], "float32")
+SEMAPHORES = (["V", "A", "P", "I", "dsl", "dpa", "dx0", "dx1", "dx23", "dx4", "dw0", "dw12", "dw34", "dy012", "dy3", "dy4"]
+              + ["ca%d" % t for t in range(1, 5)] + ["sa%d" % t for t in range(1, 5)] + ["ls%d" % t for t in range(4)])
+
+
+def rank_program(g, core, T, topo):
+    rank = T.rank_of(core)
+    if rank is None:
+        return
+    S = T.sem
+    Copy = ActivationFunctionType.Copy
+    queues = {"V": g.vector, "A": g.scalar, "P": g.tensor, "G": g, "Y": g.sync}
+    count = {"V": 0, "A": 0, "P": 0}
+    seen = {q: {} for q in queues}
+
+    def wait(q, *deps):
+        for sem, val in deps:
+            if seen[q].get(sem, 0) < val:
+                queues[q].wait_ge(S[sem], val)
+                seen[q][sem] = val
+
+    def done(q, ins):
+        count[q] += 1
+        ins.then_inc(S[q], 1)
+        return (q, count[q])
+
+    def load(q, sem, out, in_):
+        queues[q].dma_start(out, in_).then_inc(S[sem], 16)
+
+    def xcols(a, b):
+        return slice(512 * a, 512 * b)
+
+    load("Y", "dx0", T.xt[:, xcols(0, 1)], T.x[:, xcols(0, 1)])
+    for h in range(4):
+        load("Y", "dsl", T.slw[16 * h:16 * h + 16, :], T.sl[:, :])
+        load("A", "dsl", T.slw[16 * h + 64:16 * h + 80, :], T.sl[:, :])
+    for h in range(4):
+        load("Y", "dpa", T.paw[16 * h:16 * h + 16, :], T.pa[:, :])
+        load("A", "dpa", T.paw[16 * h + 64:16 * h + 80, :], T.pa[:, :])
+    load("Y", "dx1", T.xt[:, xcols(1, 2)], T.x[:, xcols(1, 2)])
+    load("Y", "dx23", T.xt[:, xcols(2, 4)], T.x[:, xcols(2, 4)])
+    load("Y", "dw0", T.wt[:, xcols(0, 1)], T.w[:, xcols(0, 1)])
+    SL, PA = ("dsl", 128), ("dpa", 128)
+    x_in = {0: ("dx0", 16), 1: ("dx1", 16), 2: ("dx23", 16), 3: ("dx23", 16), 4: ("dx4", 16)}
+    w_in = {0: ("dw0", 16), 1: ("dw12", 16), 2: ("dw12", 16), 3: ("dw34", 16), 4: ("dw34", 16)}
+
+    g.iota(T.part[:, :], [[0, 32]], 0, 1).then_inc(S.I, 1)
+    g.iota(T.base[:, :], [[0, 4], [16, 8]], 257, 0).then_inc(S.I, 1)
+    g.iota(T.even[:, :], [[2, 12], [0, 2]], 0, 0).then_inc(S.I, 1)
+    wait("V", ("I", 3))
+    t_low = done("V", g.vector.tensor_scalar(T.low[:, :], T.part[:, :], 15, None, AluOpType.bitwise_and))
+    t_odd = done("V", g.vector.tensor_scalar(T.odd[:, :], T.part[:, 0:24], 4, 1, AluOpType.logical_shift_right, AluOpType.bitwise_and))
+    wait("V", t_low)
+    t_fresh = done("V", g.vector.tensor_tensor(T.fresh[:, :], T.base[:, :], T.low[:, :], AluOpType.add))
+    wait("V", t_odd)
+    t_rep32 = done("V", g.vector.tensor_tensor(T.rep32[:, :], T.even[:, :], T.odd[:, :], AluOpType.add))
+    wait("V", t_rep32)
+    t_rep = done("V", g.vector.tensor_copy(T.rep[:, :], T.rep32[:, :]))
+
+    others = [d for d in range(N) if d != rank]
+    lo, hi = others[0], others[-1] + 1
+    runs = []
+    for i, d in enumerate(others):
+        if runs and runs[-1][1] + runs[-1][2] == d:
+            runs[-1] = (runs[-1][0], runs[-1][1], runs[-1][2] + 1)
+        else:
+            runs.append((i, d, 1))
+
+    def share(d, scales):
+        e = topo.engines(core, T.cores[d])
+        half, step = len(e) // 2, (d - rank) % N
+        first, second = (e[half:], e[:half]) if scales else (e[:half], e[half:])
+        return first if step == 1 else second[:half // 2] if step == 2 else second[half // 2:]
+
+    def bits(e):
+        return sum(1 << k for k in e)
+
+    arrive = sum(len(topo.engines(core, T.cores[d])) // (2 if (rank - d) % N == 1 else 4) for d in others)
+
+    def send(t, scales):
+        transfers = []
+        for i, d in enumerate(others):
+            rid, pid = topo.addr(T.cores[d], core)
+            a, b = 128 + CAPP * rank, 160 + CAPP * rank
+            if scales:
+                src, dst = T["sp%d" % t][:, CAPP * i:CAPP * i + CAPP], T["p%d" % (t + 1)][:, a:b]
+            else:
+                src = T["sc%d" % t][:, CAPP * i:CAPP * i + CAPP].bitcast(dt.uint8)
+                dst = T["c%d" % (t + 1)][:, a:b].bitcast(dt.uint8)
+            transfers.append(RemoteDMATransfer(dst_ids=[DstId(rid=rid, pnc=pid)], dma_engine_mask=bits(share(d, scales)),
+                                               remote_sem=S["%s%d" % ("sa" if scales else "ca", t + 1)], srcs=[src], dsts=[dst]))
+        g.remote_dma_fused(transfers, local_sem=S["ls%d" % t])
+
+    left = 2 * sum(len(share(d, False)) for d in others)
+
+    def pick_codes(dst, a, b, src, n, off, deps):
+        wait("V", *deps)
+        return done("V", g.vector.tensor_copy(T[dst][:, a:b].bitcast(dt.uint32), T[src][:, 0:n].bitcast(dt.uint32).indirect(off)))
+
+    def pick_scales(dst, a, b, src, n, off, deps):
+        wait("A", *deps)
+        return done("A", g.scalar.activation(T[dst][:, a:b], T[src][:, 0:n].indirect(off), Copy))
+
+    def quantise(c, p, a, tile, i, dep):
+        wait("V", dep)
+        return done("V", g.vector.quantize_mx(T[c][:, a:a + 128], T[p][:, a:a + 128], T[tile][:, xcols(i, i + 1)]))
+
+    q_w = {}
+
+    def product(t, codes, plane, deps):
+        wait("P", q_w[t], *deps)
+        return done("P", g.tensor.matmul_mx(T.ps[:, 512 * t:512 * t + 128], T.wc[:, 128 * t:128 * t + 128], T.wp[:, 128 * t:128 * t + 128],
+                                            T[codes][:, 0:128], T[plane][:, 0:128], True, True))
+
+    def out_block(t, dep):
+        wait("A", dep)
+        return done("A", g.scalar.activation(T.ysb[:, 128 * t:128 * t + 128], T.ps[:, 512 * t:512 * t + 128], Copy))
+
+    def compose(t):
+        ga, lin, gb, tb = (T["%s%d" % (s, t)] for s in ("ga", "lin", "gb", "tb"))
+        wait("V", t_rep, t_pav)
+        k = done("V", g.vector.tensor_copy(ga[:, :], T.pav[:, 0:32].indirect(T.rep[:, 8 * t - 8:8 * t])))
+        wait("V", k)
+        k = done("V", g.vector.transpose(lin[:, :], ga[:, :]))
+        wait("V", k, t_sd)
+        n = 64 * (hi - lo)
+        k = done("V", g.vector.tensor_copy(gb[:, 0:n], lin[:, 0:128].indirect(T.sd[:, 16 * t + 4 * lo:16 * t + 4 * hi])))
+        wait("V", k)
+        k = done("V", g.vector.transpose(tb[:, 0:n], gb[:, 0:n]))
+        wait("V", k)
+        for i, d, m in runs:
+            k = done("V", g.vector.tensor_copy(T["off%d" % t][:, 2 * i:2 * (i + m)], tb[:, 64 * (d - lo):64 * (d - lo + m):32]))
+        return k
+
+    wait("V", SL)
+    for i, d, m in runs:
+        t_off = done("V", g.vector.tensor_copy(T.off0[:, 2 * i:2 * (i + m)], T.slw[:, 2 * d:2 * (d + m)]))
+    q_k0 = quantise("k0c", "k0p", 0, "xt", 0, x_in[0])
+    s_c = pick_codes("sc0", 0, 96, "k0c", 128, T.off0[:, 0:6], [t_off, q_k0])
+    s_p = pick_scales("sp0", 0, 96, "k0p", 128, T.off0[:, 0:6], [t_off, q_k0])
+    wait("G", s_c)
+    send(0, False)
+    wait("G", s_p)
+    send(0, True)
+
+    for h in range(2):
+        t_sd = done("V", g.vector.tensor_copy(T.sd[:, h:64:2], T.slw[:, :]))
+    wait("V", PA)
+    k = done("V", g.vector.tensor_scalar(T.neg[:, :], T.paw[:, :], 0, None, AluOpType.is_lt))
+    wait("V", k, t_fresh)
+    k = done("V", g.vector.tensor_tensor(T.add[:, :], T.neg[:, :], T.fresh[:, :], AluOpType.mult))
+    wait("V", k)
+    t_pav = done("V", g.vector.tensor_tensor(T.pav[:, :], T.paw[:, :], T.add[:, :], AluOpType.add))
+    t_off = compose(1)
+    t_pao = done("V", g.vector.tensor_copy(T.paoff[:, :], T.pav[:, :]))
+    q_k = quantise("c1", "p1", 0, "xt", 0, x_in[0])
+    q_p = quantise("c1", "p1", 256, "xt", 1, x_in[1])
+    kc, kp = q_k, q_k
+
+    stored = {}
+    for t in range(1, 5):
+        codes, plane = "c%d" % t, "p%d" % t
+        nc, np_ = ("c%d" % (t + 1), "p%d" % (t + 1)) if t < 4 else ("k4c", "k4p")
+        pao = T.paoff[:, 8 * t - 8:8 * t]
+        here_c = [t_off, t_pao, kc, q_p, ("ca%d" % t, arrive)]
+        here_p = [t_off, t_pao, kp, q_p, ("sa%d" % t, arrive)]
+        old = (kc, kp)
+        if t < 4:
+            off = T["off%d" % t][:, 0:6]
+            s_c = pick_codes("sc%d" % t, 0, 96, codes, 384, off, here_c)
+            s_p = pick_scales("sp%d" % t, 0, 96, plane, 384, off, here_p)
+            wait("G", s_c)
+            send(t, False)
+            wait("G", s_p)
+            send(t, True)
+        kc = pick_codes(nc, 0, 128, codes, 384, pao, here_c)
+        kp = pick_scales(np_, 0, 128, plane, 384, pao, here_p)
+        if t < 4:
+            q_p = quantise("c%d" % (t + 1), "p%d" % (t + 1), 256, "xt", t + 1, x_in[t + 1])
+        if t < 3:
+            t_off = compose(t + 1)
+        for i in {1: [0], 2: [1, 2], 3: [3, 4], 4: []}[t]:
+            q_w[i] = quantise("wc", "wp", 128 * i, "wt", i, w_in[i])
+        if t == 1:
+            stored[0] = out_block(0, product(0, "c1", "p1", old))
+        if t == 2:
+            stored[1] = out_block(1, product(1, "c2", "p2", old))
+            stored[2] = out_block(2, product(2, "c3", "p3", (kc, kp)))
+        if t == 3:
+            stored[3] = out_block(3, product(3, "c4", "p4", (kc, kp)))
+    m4 = product(4, "k4c", "k4p", (kc, kp))
+    wait("V", m4)
+    last = done("V", g.vector.tensor_copy(T.ysb[:, 512:640], T.ps[:, 2048:2176]))
+
+    wait("Y", ("ls0", left))
+    load("Y", "dx4", T.xt[:, xcols(4, 5)], T.x[:, xcols(4, 5)])
+    load("Y", "dw12", T.wt[:, xcols(1, 3)], T.w[:, xcols(1, 3)])
+    wait("Y", ("ls1", left))
+    load("Y", "dw34", T.wt[:, xcols(3, 5)], T.w[:, xcols(3, 5)])
+    wait("Y", ("ls2", left), stored[2])
+    load("Y", "dy012", T.y[:, 0:384], T.ysb[:, 0:384])
+    wait("Y", ("ls3", left), stored[3])
+    load("Y", "dy3", T.y[:, 384:512], T.ysb[:, 384:512])
+    wait("Y", last)
+    load("Y", "dy4", T.y[:, 512:640], T.ysb[:, 512:640])
+    wait("Y", ("dy012", 16), ("dy3", 16), ("dy4", 16))

@@ -9,10 +9,12 @@ SCRATCH = {
     "base": ("sbuf", [128, 32], "int32"), "part": ("sbuf", [128, 32], "int32"), "low": ("sbuf", [128, 32], "int32"),
     "fresh": ("sbuf", [128, 32], "int32"), "even": ("sbuf", [128, 24], "int32"), "odd": ("sbuf", [128, 24], "int32"),
     "rep32": ("sbuf", [128, 24], "int32"), "rep": ("sbuf", [128, 24], "uint16"),
-    "neg": ("sbuf", [128, 32], "int32"), "add": ("sbuf", [128, 32], "int32"), "pav": ("sbuf", [128, 32], "int32"),
-    "paoff": ("sbuf", [128, 32], "uint16"), "sd": ("sbuf", [128, 64], "uint16"),
+    "pam": ("sbuf", [128, 32], "int32"), "pav": ("sbuf", [128, 32], "float32"),
+    "paoff": ("sbuf", [128, 32], "uint16"), "sd": ("sbuf", [128, 24], "uint16"),
+    "ga": ("sbuf", [128, 384], "bfloat16"), "lin": ("sbuf", [128, 384], "bfloat16"),
+    "gb": ("sbuf", [128, 288], "bfloat16"), "tb": ("sbuf", [128, 288], "bfloat16"),
     "k0c": ("sbuf", [128, 128], CODE), "k0p": ("sbuf", [128, 128], PLANE),
-    "k4c": ("sbuf", [128, 128], CODE), "k4p": ("sbuf", [128, 128], PLANE),
+    "c5": ("sbuf", [128, 128], CODE), "p5": ("sbuf", [128, 128], PLANE),
     "wc": ("sbuf", [128, 640], CODE), "wp": ("sbuf", [128, 640], PLANE),
     "ysb": ("sbuf", [128, 640], "float32"), "ps": ("psum", [128, 2560], "float32"),
 }
@@ -20,16 +22,11 @@ for _t in range(1, 5):
     SCRATCH["c%d" % _t] = ("sbuf", [128, 384], CODE)
     SCRATCH["p%d" % _t] = ("sbuf", [128, 384], PLANE)
 for _t in range(4):
-    SCRATCH["sc%d" % _t] = ("sbuf", [128, 96], CODE)
-    SCRATCH["sp%d" % _t] = ("sbuf", [128, 96], PLANE)
-    SCRATCH["off%d" % _t] = ("sbuf", [128, 6], "uint16")
-for _t in range(1, 4):
-    SCRATCH["ga%d" % _t] = ("sbuf", [128, 128], "float32")
-    SCRATCH["lin%d" % _t] = ("sbuf", [128, 128], "float32")
-    SCRATCH["gb%d" % _t] = ("sbuf", [128, 256], "float32")
-    SCRATCH["tb%d" % _t] = ("sbuf", [128, 256], "float32")
-SEMAPHORES = (["V", "A", "P", "I", "dsl", "dpa", "dx0", "dx1", "dx23", "dx4", "dw0", "dw12", "dw34", "dy012", "dy3", "dy4"]
-              + ["ca%d" % t for t in range(1, 5)] + ["sa%d" % t for t in range(1, 5)] + ["ls%d" % t for t in range(4)])
+    SCRATCH["sc%d" % _t] = ("sbuf", [128, 128], CODE)
+    SCRATCH["sp%d" % _t] = ("sbuf", [128, 128], PLANE)
+    SCRATCH["off%d" % _t] = ("sbuf", [128, 8], "uint16")
+SEMAPHORES = (["V", "A", "P", "I", "dsl", "dsl2", "dpa", "dx0", "dx1", "dx24", "dw02", "dw34", "dy03", "dy4", "lc1", "lx"]
+              + ["ca%d" % t for t in range(1, 5)] + ["sa%d" % t for t in range(1, 5)])
 
 
 def rank_program(g, core, T, topo):
@@ -37,7 +34,7 @@ def rank_program(g, core, T, topo):
     if rank is None:
         return
     S = T.sem
-    Copy = ActivationFunctionType.Copy
+    Copy, Identity = ActivationFunctionType.Copy, ActivationFunctionType.Identity
     queues = {"V": g.vector, "A": g.scalar, "P": g.tensor, "G": g, "Y": g.sync}
     count = {"V": 0, "A": 0, "P": 0}
     seen = {q: {} for q in queues}
@@ -59,177 +56,174 @@ def rank_program(g, core, T, topo):
     def xcols(a, b):
         return slice(512 * a, 512 * b)
 
+    def group(h):
+        return slice(16 * h, 16 * h + 16)
+
+    load("Y", "dsl", T.slw[group(0), 0:8], T.sl[:, 0:8])
+    load("A", "dsl", T.slw[group(1), 0:8], T.sl[:, 0:8])
     load("Y", "dx0", T.xt[:, xcols(0, 1)], T.x[:, xcols(0, 1)])
-    for h in range(4):
-        load("Y", "dsl", T.slw[16 * h:16 * h + 16, :], T.sl[:, :])
-        load("A", "dsl", T.slw[16 * h + 64:16 * h + 80, :], T.sl[:, :])
-    for h in range(4):
-        load("Y", "dpa", T.paw[16 * h:16 * h + 16, :], T.pa[:, :])
-        load("A", "dpa", T.paw[16 * h + 64:16 * h + 80, :], T.pa[:, :])
+    for h in range(8):
+        load("Y" if h < 3 else "A", "dpa", T.paw[group(h), :], T.pa[:, :])
     load("Y", "dx1", T.xt[:, xcols(1, 2)], T.x[:, xcols(1, 2)])
-    load("Y", "dx23", T.xt[:, xcols(2, 4)], T.x[:, xcols(2, 4)])
-    load("Y", "dw0", T.wt[:, xcols(0, 1)], T.w[:, xcols(0, 1)])
-    SL, PA = ("dsl", 128), ("dpa", 128)
-    x_in = {0: ("dx0", 16), 1: ("dx1", 16), 2: ("dx23", 16), 3: ("dx23", 16), 4: ("dx4", 16)}
-    w_in = {0: ("dw0", 16), 1: ("dw12", 16), 2: ("dw12", 16), 3: ("dw34", 16), 4: ("dw34", 16)}
+    for h in range(8):
+        load("YA"[h % 2], "dsl2", T.slw[group(h), 8:31], T.sl[:, 8 + h % 2:31 + h % 2])
+    load("Y", "dx24", T.xt[:, xcols(2, 5)], T.x[:, xcols(2, 5)])
+    load("Y", "dw02", T.wt[:, xcols(0, 3)], T.w[:, xcols(0, 3)])
+    SL, SL2, PA = ("dsl", 32), ("dsl2", 128), ("dpa", 128)
+    x_in = {0: ("dx0", 16), 1: ("dx1", 16), 2: ("dx24", 16), 3: ("dx24", 16), 4: ("dx24", 16)}
+    w_in = {0: ("dw02", 16), 1: ("dw02", 16), 2: ("dw02", 16), 3: ("dw34", 16), 4: ("dw34", 16)}
 
     g.iota(T.part[:, :], [[0, 32]], 0, 1).then_inc(S.I, 1)
-    g.iota(T.base[:, :], [[0, 4], [16, 8]], 257, 0).then_inc(S.I, 1)
     g.iota(T.even[:, :], [[2, 12], [0, 2]], 0, 0).then_inc(S.I, 1)
-    wait("V", ("I", 3))
-    t_low = done("V", g.vector.tensor_scalar(T.low[:, :], T.part[:, :], 15, None, AluOpType.bitwise_and))
+    g.iota(T.base[:, :], [[0, 4], [16, 8]], 256, 0).then_inc(S.I, 1)
+    wait("V", ("I", 1))
     t_odd = done("V", g.vector.tensor_scalar(T.odd[:, :], T.part[:, 0:24], 4, 1, AluOpType.logical_shift_right, AluOpType.bitwise_and))
-    wait("V", t_low)
-    t_fresh = done("V", g.vector.tensor_tensor(T.fresh[:, :], T.base[:, :], T.low[:, :], AluOpType.add))
-    wait("V", t_odd)
+    t_low = done("V", g.vector.tensor_scalar(T.low[:, :], T.part[:, :], 15, None, AluOpType.bitwise_and))
+    wait("V", ("I", 2), t_odd)
     t_rep32 = done("V", g.vector.tensor_tensor(T.rep32[:, :], T.even[:, :], T.odd[:, :], AluOpType.add))
-    wait("V", t_rep32)
-    t_rep = done("V", g.vector.tensor_copy(T.rep[:, :], T.rep32[:, :]))
 
-    others = [d for d in range(N) if d != rank]
-    lo, hi = others[0], others[-1] + 1
-    runs = []
-    for i, d in enumerate(others):
-        if runs and runs[-1][1] + runs[-1][2] == d:
-            runs[-1] = (runs[-1][0], runs[-1][1], runs[-1][2] + 1)
-        else:
-            runs.append((i, d, 1))
+    twin = rank ^ 1
+    others = [d for d in range(N) if d // 2 != rank // 2] + [twin]
+    runs = [(0, others[0], 2), (2, twin, 1)]
 
-    def share(d, scales):
-        e = topo.engines(core, T.cores[d])
-        half, step = len(e) // 2, (d - rank) % N
-        first, second = (e[half:], e[:half]) if scales else (e[:half], e[half:])
-        return first if step == 1 else second[:half // 2] if step == 2 else second[half // 2:]
+    def share(r, d, t, scales):
+        e = topo.engines(T.cores[r], T.cores[d])
+        first, second = (e[1::2], e[0::2]) if scales else (e[0::2], e[1::2])
+        half = len(second) // 2
+        return first if d == r ^ 1 else second[half * (d % 2):half * (d % 2 + 1)]
 
     def bits(e):
         return sum(1 << k for k in e)
 
-    arrive = sum(len(topo.engines(core, T.cores[d])) // (2 if (rank - d) % N == 1 else 4) for d in others)
+    def arrive(t, scales):
+        return "%s%d" % ("sa" if scales else "ca", t), sum(len(share(s, rank, t, scales)) for s in others)
 
-    def send(t, scales):
+    def left(t, scales):
+        return sum(len(share(rank, d, t, scales)) for d in others)
+
+    def send(t, scales, run, dep):
         transfers = []
-        for i, d in enumerate(others):
+        for i in range(run[0], run[0] + run[2]):
+            d = others[i]
             rid, pid = topo.addr(T.cores[d], core)
             a, b = 128 + CAPP * rank, 160 + CAPP * rank
+            s = CAPP * i
             if scales:
-                src, dst = T["sp%d" % t][:, CAPP * i:CAPP * i + CAPP], T["p%d" % (t + 1)][:, a:b]
+                src, dst = T["sp%d" % (t - 1)][:, s:s + CAPP], T["p%d" % t][:, a:b]
             else:
-                src = T["sc%d" % t][:, CAPP * i:CAPP * i + CAPP].bitcast(dt.uint8)
-                dst = T["c%d" % (t + 1)][:, a:b].bitcast(dt.uint8)
-            transfers.append(RemoteDMATransfer(dst_ids=[DstId(rid=rid, pnc=pid)], dma_engine_mask=bits(share(d, scales)),
-                                               remote_sem=S["%s%d" % ("sa" if scales else "ca", t + 1)], srcs=[src], dsts=[dst]))
-        g.remote_dma_fused(transfers, local_sem=S["ls%d" % t])
-
-    left = 2 * sum(len(share(d, False)) for d in others)
+                src = T["sc%d" % (t - 1)][:, s:s + CAPP].bitcast(dt.uint8)
+                dst = T["c%d" % t][:, a:b].bitcast(dt.uint8)
+            transfers.append(RemoteDMATransfer(dst_ids=[DstId(rid=rid, pnc=pid)], dma_engine_mask=bits(share(rank, d, t, scales)),
+                                               remote_sem=S["%s%d" % ("sa" if scales else "ca", t)], srcs=[src], dsts=[dst]))
+        wait("G", dep)
+        g.remote_dma_fused(transfers, local_sem=S["lc1" if t == 1 and not scales else "lx"])
 
     def pick_codes(dst, a, b, src, n, off, deps):
         wait("V", *deps)
         return done("V", g.vector.tensor_copy(T[dst][:, a:b].bitcast(dt.uint32), T[src][:, 0:n].bitcast(dt.uint32).indirect(off)))
 
-    def pick_scales(dst, a, b, src, n, off, deps):
-        wait("A", *deps)
-        return done("A", g.scalar.activation(T[dst][:, a:b], T[src][:, 0:n].indirect(off), Copy))
+    def gather(q, out, window, deps):
+        wait(q, *deps)
+        return done(q, g.vector.tensor_copy(out, window) if q == "V" else g.scalar.activation(out, window, Copy))
 
     def quantise(c, p, a, tile, i, dep):
         wait("V", dep)
         return done("V", g.vector.quantize_mx(T[c][:, a:a + 128], T[p][:, a:a + 128], T[tile][:, xcols(i, i + 1)]))
 
-    q_w = {}
+    def pick_and_send(t, codes, plane, n, off, here_c, here_p):
+        for scales in (False, True):
+            for run, o in zip(runs, off):
+                a, b = CAPP * run[0], CAPP * (run[0] + run[2])
+                send(t, scales, run, gather("A", T["sp%d" % (t - 1)][:, a:b], T[plane][:, 0:n].indirect(o), here_p) if scales
+                     else pick_codes("sc%d" % (t - 1), a, b, codes, n, o, here_c))
 
-    def product(t, codes, plane, deps):
-        wait("P", q_w[t], *deps)
+    q_w, made = {}, {}
+
+    def product(t):
+        wait("P", q_w[t], *made[t])
         return done("P", g.tensor.matmul_mx(T.ps[:, 512 * t:512 * t + 128], T.wc[:, 128 * t:128 * t + 128], T.wp[:, 128 * t:128 * t + 128],
-                                            T[codes][:, 0:128], T[plane][:, 0:128], True, True))
+                                            T["c%d" % (t + 1)][:, 0:128], T["p%d" % (t + 1)][:, 0:128], True, True))
 
-    def out_block(t, dep):
-        wait("A", dep)
+    def out_block(t):
+        wait("A", product(t))
         return done("A", g.scalar.activation(T.ysb[:, 128 * t:128 * t + 128], T.ps[:, 512 * t:512 * t + 128], Copy))
 
-    def compose(t):
-        ga, lin, gb, tb = (T["%s%d" % (s, t)] for s in ("ga", "lin", "gb", "tb"))
-        wait("V", t_rep, t_pav)
-        k = done("V", g.vector.tensor_copy(ga[:, :], T.pav[:, 0:32].indirect(T.rep[:, 8 * t - 8:8 * t])))
-        wait("V", k)
-        k = done("V", g.vector.transpose(lin[:, :], ga[:, :]))
-        wait("V", k, t_sd)
-        n = 64 * (hi - lo)
-        k = done("V", g.vector.tensor_copy(gb[:, 0:n], lin[:, 0:128].indirect(T.sd[:, 16 * t + 4 * lo:16 * t + 4 * hi])))
-        wait("V", k)
-        k = done("V", g.vector.transpose(tb[:, 0:n], gb[:, 0:n]))
-        wait("V", k)
+    def spread(a, b):
+        wait("A", t_rep, t_pav)
+        return done("A", g.scalar.activation(T.ga[:, 128 * a:128 * b], T.pav[:, 0:32].indirect(T.rep[:, 8 * a:8 * b]), Identity, bias=-128.0))
+
+    def turn(out, in_, a, b, dep):
+        wait("V", dep)
+        return done("V", g.vector.transpose(out[:, a:b], in_[:, a:b]))
+
+    def through(q, t, dep):
         for i, d, m in runs:
-            k = done("V", g.vector.tensor_copy(T["off%d" % t][:, 2 * i:2 * (i + m)], tb[:, 64 * (d - lo):64 * (d - lo + m):32]))
+            k = gather(q, T.gb[:, 96 * t - 96 + 32 * i:96 * t - 96 + 32 * (i + m)],
+                       T.lin[:, 128 * t - 128:128 * t].indirect(T.sd[:, 8 * t - 8 + 2 * d:8 * t - 8 + 2 * (d + m)]), [dep, t_sd])
         return k
 
-    wait("V", SL)
-    for i, d, m in runs:
-        t_off = done("V", g.vector.tensor_copy(T.off0[:, 2 * i:2 * (i + m)], T.slw[:, 2 * d:2 * (d + m)]))
-    q_k0 = quantise("k0c", "k0p", 0, "xt", 0, x_in[0])
-    s_c = pick_codes("sc0", 0, 96, "k0c", 128, T.off0[:, 0:6], [t_off, q_k0])
-    s_p = pick_scales("sp0", 0, 96, "k0p", 128, T.off0[:, 0:6], [t_off, q_k0])
-    wait("G", s_c)
-    send(0, False)
-    wait("G", s_p)
-    send(0, True)
+    def table(t, dep):
+        wait("V", turn(T.tb, T.gb, 96 * t - 96, 96 * t, dep))
+        return done("V", g.vector.tensor_scalar(T["off%d" % t][:, 0:6], T.tb[:, 96 * t - 96:96 * t:16], 128.0, None, AluOpType.add))
 
-    for h in range(2):
-        t_sd = done("V", g.vector.tensor_copy(T.sd[:, h:64:2], T.slw[:, :]))
-    wait("V", PA)
-    k = done("V", g.vector.tensor_scalar(T.neg[:, :], T.paw[:, :], 0, None, AluOpType.is_lt))
+    wait("V", SL)
+    for a in range(0, 128, 32):
+        t_off = done("V", g.vector.tensor_copy(T.off0[a:a + 32, :], T.slw[0:32, 0:8]))
+    q_k0 = quantise("k0c", "k0p", 0, "xt", 0, x_in[0])
+    pick_and_send(1, "k0c", "k0p", 128, [T.off0[:, 2 * d:2 * (d + m)] for i, d, m in runs], [t_off, q_k0], [t_off, q_k0])
+
+    wait("V", ("I", 3), t_low, t_rep32, PA)
+    k = done("V", g.vector.tensor_scalar(T.pam[:, :], T.paw[:, :], 511, None, AluOpType.bitwise_and))
+    t_fresh = done("V", g.vector.tensor_tensor(T.fresh[:, :], T.base[:, :], T.low[:, :], AluOpType.add))
+    t_rep = done("V", g.vector.tensor_copy(T.rep[:, :], T.rep32[:, :]))
     wait("V", k, t_fresh)
-    k = done("V", g.vector.tensor_tensor(T.add[:, :], T.neg[:, :], T.fresh[:, :], AluOpType.mult))
-    wait("V", k)
-    t_pav = done("V", g.vector.tensor_tensor(T.pav[:, :], T.paw[:, :], T.add[:, :], AluOpType.add))
-    t_off = compose(1)
-    t_pao = done("V", g.vector.tensor_copy(T.paoff[:, :], T.pav[:, :]))
+    t_pav = done("V", g.vector.tensor_tensor(T.pav[:, :], T.pam[:, :], T.fresh[:, :], AluOpType.min))
+    t_ga = spread(0, 1)
+    wait("V", SL2)
+    for h in range(2):
+        t_sd = done("V", g.vector.tensor_copy(T.sd[:, h:24:2], T.slw[:, 8:32:2]))
     q_k = quantise("c1", "p1", 0, "xt", 0, x_in[0])
+    t_gb = through("A", 1, turn(T.lin, T.ga, 0, 128, t_ga))
+    t_ga = spread(1, 3)
+    wait("V", t_pav)
+    t_pao = done("V", g.vector.tensor_copy(T.paoff[:, :], T.pav[:, :]))
     q_p = quantise("c1", "p1", 256, "xt", 1, x_in[1])
-    kc, kp = q_k, q_k
+    t_off = table(1, t_gb)
+    made[0] = (q_k,)
 
     stored = {}
-    for t in range(1, 5):
+    for t in range(1, 4):
         codes, plane = "c%d" % t, "p%d" % t
-        nc, np_ = ("c%d" % (t + 1), "p%d" % (t + 1)) if t < 4 else ("k4c", "k4p")
-        pao = T.paoff[:, 8 * t - 8:8 * t]
-        here_c = [t_off, t_pao, kc, q_p, ("ca%d" % t, arrive)]
-        here_p = [t_off, t_pao, kp, q_p, ("sa%d" % t, arrive)]
-        old = (kc, kp)
-        if t < 4:
-            off = T["off%d" % t][:, 0:6]
-            s_c = pick_codes("sc%d" % t, 0, 96, codes, 384, off, here_c)
-            s_p = pick_scales("sp%d" % t, 0, 96, plane, 384, off, here_p)
-            wait("G", s_c)
-            send(t, False)
-            wait("G", s_p)
-            send(t, True)
-        kc = pick_codes(nc, 0, 128, codes, 384, pao, here_c)
-        kp = pick_scales(np_, 0, 128, plane, 384, pao, here_p)
-        if t < 4:
-            q_p = quantise("c%d" % (t + 1), "p%d" % (t + 1), 256, "xt", t + 1, x_in[t + 1])
-        if t < 3:
-            t_off = compose(t + 1)
-        for i in {1: [0], 2: [1, 2], 3: [3, 4], 4: []}[t]:
-            q_w[i] = quantise("wc", "wp", 128 * i, "wt", i, w_in[i])
+        off, pao = [T["off%d" % t][:, 2 * i:2 * (i + m)] for i, d, m in runs], T.paoff[:, 8 * t - 8:8 * t]
+        here = [t_off, t_pao, q_p]
+        here_c, here_p = here + [made[t - 1][0], arrive(t, False)], here + [made[t - 1][-1], arrive(t, True)]
+        pick_and_send(t + 1, codes, plane, 384, off, here_c, here_p)
+        made[t] = (pick_codes("c%d" % (t + 1), 0, 128, codes, 384, pao, here_c),
+                   gather("A", T["p%d" % (t + 1)][:, 0:128], T[plane][:, 0:384].indirect(pao), here_p))
         if t == 1:
-            stored[0] = out_block(0, product(0, "c1", "p1", old))
+            t_lin = turn(T.lin, T.ga, 128, 384, t_ga)
+            t_off = table(2, through("V", 2, t_lin))
+            t_gb = through("A", 3, t_lin)
         if t == 2:
-            stored[1] = out_block(1, product(1, "c2", "p2", old))
-            stored[2] = out_block(2, product(2, "c3", "p3", (kc, kp)))
-        if t == 3:
-            stored[3] = out_block(3, product(3, "c4", "p4", (kc, kp)))
-    m4 = product(4, "k4c", "k4p", (kc, kp))
-    wait("V", m4)
+            t_off = table(3, t_gb)
+        q_p = quantise("c%d" % (t + 1), "p%d" % (t + 1), 256, "xt", t + 1, x_in[t + 1])
+        for i in {1: [0], 2: [1, 2], 3: [3, 4]}[t]:
+            q_w[i] = quantise("wc", "wp", 128 * i, "wt", i, w_in[i])
+        for i in {1: [], 2: [0], 3: [1, 2, 3]}[t]:
+            stored[i] = out_block(i)
+
+    halves = [(0, 64, T.paoff[:, 24:28]), (64, 128, T.paoff[:, 28:32])]
+    for a, b, pao in halves:
+        kc = pick_codes("c5", a, b, "c4", 384, pao, [q_p, made[3][0], arrive(R, False)])
+    made[4] = [kc] + [gather(q, T.p5[:, a:b], T.p4[:, 0:384].indirect(pao), [q_p, made[3][1], arrive(R, True)])
+                      for q, (a, b, pao) in zip("AV", halves)]
+    wait("V", product(4))
     last = done("V", g.vector.tensor_copy(T.ysb[:, 512:640], T.ps[:, 2048:2176]))
 
-    wait("Y", ("ls0", left))
-    load("Y", "dx4", T.xt[:, xcols(4, 5)], T.x[:, xcols(4, 5)])
-    load("Y", "dw12", T.wt[:, xcols(1, 3)], T.w[:, xcols(1, 3)])
-    wait("Y", ("ls1", left))
+    wait("Y", ("lc1", left(1, False)))
     load("Y", "dw34", T.wt[:, xcols(3, 5)], T.w[:, xcols(3, 5)])
-    wait("Y", ("ls2", left), stored[2])
-    load("Y", "dy012", T.y[:, 0:384], T.ysb[:, 0:384])
-    wait("Y", ("ls3", left), stored[3])
-    load("Y", "dy3", T.y[:, 384:512], T.ysb[:, 384:512])
+    wait("Y", ("lx", sum(left(t, k) for t in range(1, R + 1) for k in (False, True)) - left(1, False)), stored[3])
+    load("Y", "dy03", T.y[:, 0:512], T.ysb[:, 0:512])
     wait("Y", last)
     load("Y", "dy4", T.y[:, 512:640], T.ysb[:, 512:640])
-    wait("Y", ("dy012", 16), ("dy3", 16), ("dy4", 16))
+    wait("Y", ("dy03", 16), ("dy4", 16))

from concourse.bass import DstId, RemoteDMATransfer
from concourse.mybir import dt, AluOpType, ActivationFunctionType

CODE, PLANE = "float8_e4m3fn_x4", "uint8"
N, C, R, CAPP = 4, 128, 4, 32
SCRATCH = {
    "xt": ("sbuf", [128, 2560], "bfloat16"), "wt": ("sbuf", [128, 2560], "bfloat16"),
    "slw": ("sbuf", [128, 32], "int32"), "paw": ("sbuf", [128, 32], "int32"),
    "base": ("sbuf", [128, 32], "int32"), "part": ("sbuf", [128, 32], "int32"), "low": ("sbuf", [128, 32], "int32"),
    "fresh": ("sbuf", [128, 32], "int32"), "even": ("sbuf", [128, 24], "int32"), "odd": ("sbuf", [128, 24], "int32"),
    "rep32": ("sbuf", [128, 24], "int32"), "rep": ("sbuf", [128, 24], "uint16"),
    "pam": ("sbuf", [128, 32], "int32"), "pav": ("sbuf", [128, 32], "float32"),
    "paoff": ("sbuf", [128, 32], "uint16"), "sd": ("sbuf", [128, 24], "uint16"),
    "ga": ("sbuf", [128, 384], "bfloat16"), "lin": ("sbuf", [128, 384], "bfloat16"),
    "gb": ("sbuf", [128, 288], "bfloat16"), "tb": ("sbuf", [128, 288], "bfloat16"),
    "k0c": ("sbuf", [128, 128], CODE), "k0p": ("sbuf", [128, 128], PLANE),
    "c5": ("sbuf", [128, 128], CODE), "p5": ("sbuf", [128, 128], PLANE),
    "wc": ("sbuf", [128, 640], CODE), "wp": ("sbuf", [128, 640], PLANE),
    "ysb": ("sbuf", [128, 640], "float32"), "ps": ("psum", [128, 2560], "float32"),
}
for _t in range(1, 5):
    SCRATCH["c%d" % _t] = ("sbuf", [128, 384], CODE)
    SCRATCH["p%d" % _t] = ("sbuf", [128, 384], PLANE)
for _t in range(4):
    SCRATCH["sc%d" % _t] = ("sbuf", [128, 128], CODE)
    SCRATCH["sp%d" % _t] = ("sbuf", [128, 128], PLANE)
    SCRATCH["off%d" % _t] = ("sbuf", [128, 8], "uint16")
SEMAPHORES = (["V", "A", "P", "I", "dsl", "dsl2", "dpa", "dx0", "dx1", "dx24", "dw02", "dw34", "dy03", "dy4", "lc1", "lx"]
              + ["ca%d" % t for t in range(1, 5)] + ["sa%d" % t for t in range(1, 5)])


def rank_program(g, core, T, topo):
    rank = T.rank_of(core)
    if rank is None:
        return
    S = T.sem
    Copy, Identity = ActivationFunctionType.Copy, ActivationFunctionType.Identity
    queues = {"V": g.vector, "A": g.scalar, "P": g.tensor, "G": g, "Y": g.sync}
    count = {"V": 0, "A": 0, "P": 0}
    seen = {q: {} for q in queues}

    def wait(q, *deps):
        for sem, val in deps:
            if seen[q].get(sem, 0) < val:
                queues[q].wait_ge(S[sem], val)
                seen[q][sem] = val

    def done(q, ins):
        count[q] += 1
        ins.then_inc(S[q], 1)
        return (q, count[q])

    def load(q, sem, out, in_):
        queues[q].dma_start(out, in_).then_inc(S[sem], 16)

    def xcols(a, b):
        return slice(512 * a, 512 * b)

    def group(h):
        return slice(16 * h, 16 * h + 16)

    load("Y", "dsl", T.slw[group(0), 0:8], T.sl[:, 0:8])
    load("A", "dsl", T.slw[group(1), 0:8], T.sl[:, 0:8])
    load("Y", "dx0", T.xt[:, xcols(0, 1)], T.x[:, xcols(0, 1)])
    for h in range(8):
        load("Y" if h < 3 else "A", "dpa", T.paw[group(h), :], T.pa[:, :])
    load("Y", "dx1", T.xt[:, xcols(1, 2)], T.x[:, xcols(1, 2)])
    for h in range(8):
        load("YA"[h % 2], "dsl2", T.slw[group(h), 8:31], T.sl[:, 8 + h % 2:31 + h % 2])
    load("Y", "dx24", T.xt[:, xcols(2, 5)], T.x[:, xcols(2, 5)])
    load("Y", "dw02", T.wt[:, xcols(0, 3)], T.w[:, xcols(0, 3)])
    SL, SL2, PA = ("dsl", 32), ("dsl2", 128), ("dpa", 128)
    x_in = {0: ("dx0", 16), 1: ("dx1", 16), 2: ("dx24", 16), 3: ("dx24", 16), 4: ("dx24", 16)}
    w_in = {0: ("dw02", 16), 1: ("dw02", 16), 2: ("dw02", 16), 3: ("dw34", 16), 4: ("dw34", 16)}

    g.iota(T.part[:, :], [[0, 32]], 0, 1).then_inc(S.I, 1)
    g.iota(T.even[:, :], [[2, 12], [0, 2]], 0, 0).then_inc(S.I, 1)
    g.iota(T.base[:, :], [[0, 4], [16, 8]], 256, 0).then_inc(S.I, 1)
    wait("V", ("I", 1))
    t_odd = done("V", g.vector.tensor_scalar(T.odd[:, :], T.part[:, 0:24], 4, 1, AluOpType.logical_shift_right, AluOpType.bitwise_and))
    t_low = done("V", g.vector.tensor_scalar(T.low[:, :], T.part[:, :], 15, None, AluOpType.bitwise_and))
    wait("V", ("I", 2), t_odd)
    t_rep32 = done("V", g.vector.tensor_tensor(T.rep32[:, :], T.even[:, :], T.odd[:, :], AluOpType.add))

    twin = rank ^ 1
    others = [d for d in range(N) if d // 2 != rank // 2] + [twin]
    runs = [(0, others[0], 2), (2, twin, 1)]

    def share(r, d, t, scales):
        e = topo.engines(T.cores[r], T.cores[d])
        first, second = (e[1::2], e[0::2]) if scales else (e[0::2], e[1::2])
        half = len(second) // 2
        return first if d == r ^ 1 else second[half * (d % 2):half * (d % 2 + 1)]

    def bits(e):
        return sum(1 << k for k in e)

    def arrive(t, scales):
        return "%s%d" % ("sa" if scales else "ca", t), sum(len(share(s, rank, t, scales)) for s in others)

    def left(t, scales):
        return sum(len(share(rank, d, t, scales)) for d in others)

    def send(t, scales, run, dep):
        transfers = []
        for i in range(run[0], run[0] + run[2]):
            d = others[i]
            rid, pid = topo.addr(T.cores[d], core)
            a, b = 128 + CAPP * rank, 160 + CAPP * rank
            s = CAPP * i
            if scales:
                src, dst = T["sp%d" % (t - 1)][:, s:s + CAPP], T["p%d" % t][:, a:b]
            else:
                src = T["sc%d" % (t - 1)][:, s:s + CAPP].bitcast(dt.uint8)
                dst = T["c%d" % t][:, a:b].bitcast(dt.uint8)
            transfers.append(RemoteDMATransfer(dst_ids=[DstId(rid=rid, pnc=pid)], dma_engine_mask=bits(share(rank, d, t, scales)),
                                               remote_sem=S["%s%d" % ("sa" if scales else "ca", t)], srcs=[src], dsts=[dst]))
        wait("G", dep)
        g.remote_dma_fused(transfers, local_sem=S["lc1" if t == 1 and not scales else "lx"])

    def pick_codes(dst, a, b, src, n, off, deps):
        wait("V", *deps)
        return done("V", g.vector.tensor_copy(T[dst][:, a:b].bitcast(dt.uint32), T[src][:, 0:n].bitcast(dt.uint32).indirect(off)))

    def gather(q, out, window, deps):
        wait(q, *deps)
        return done(q, g.vector.tensor_copy(out, window) if q == "V" else g.scalar.activation(out, window, Copy))

    def quantise(c, p, a, tile, i, dep):
        wait("V", dep)
        return done("V", g.vector.quantize_mx(T[c][:, a:a + 128], T[p][:, a:a + 128], T[tile][:, xcols(i, i + 1)]))

    def pick_and_send(t, codes, plane, n, off, here_c, here_p):
        for scales in (False, True):
            for run, o in zip(runs, off):
                a, b = CAPP * run[0], CAPP * (run[0] + run[2])
                send(t, scales, run, gather("A", T["sp%d" % (t - 1)][:, a:b], T[plane][:, 0:n].indirect(o), here_p) if scales
                     else pick_codes("sc%d" % (t - 1), a, b, codes, n, o, here_c))

    q_w, made = {}, {}

    def product(t):
        wait("P", q_w[t], *made[t])
        return done("P", g.tensor.matmul_mx(T.ps[:, 512 * t:512 * t + 128], T.wc[:, 128 * t:128 * t + 128], T.wp[:, 128 * t:128 * t + 128],
                                            T["c%d" % (t + 1)][:, 0:128], T["p%d" % (t + 1)][:, 0:128], True, True))

    def out_block(t):
        wait("A", product(t))
        return done("A", g.scalar.activation(T.ysb[:, 128 * t:128 * t + 128], T.ps[:, 512 * t:512 * t + 128], Copy))

    def spread(a, b):
        wait("A", t_rep, t_pav)
        return done("A", g.scalar.activation(T.ga[:, 128 * a:128 * b], T.pav[:, 0:32].indirect(T.rep[:, 8 * a:8 * b]), Identity, bias=-128.0))

    def turn(out, in_, a, b, dep):
        wait("V", dep)
        return done("V", g.vector.transpose(out[:, a:b], in_[:, a:b]))

    def through(q, t, dep):
        for i, d, m in runs:
            k = gather(q, T.gb[:, 96 * t - 96 + 32 * i:96 * t - 96 + 32 * (i + m)],
                       T.lin[:, 128 * t - 128:128 * t].indirect(T.sd[:, 8 * t - 8 + 2 * d:8 * t - 8 + 2 * (d + m)]), [dep, t_sd])
        return k

    def table(t, dep):
        wait("V", turn(T.tb, T.gb, 96 * t - 96, 96 * t, dep))
        return done("V", g.vector.tensor_scalar(T["off%d" % t][:, 0:6], T.tb[:, 96 * t - 96:96 * t:16], 128.0, None, AluOpType.add))

    wait("V", SL)
    for a in range(0, 128, 32):
        t_off = done("V", g.vector.tensor_copy(T.off0[a:a + 32, :], T.slw[0:32, 0:8]))
    q_k0 = quantise("k0c", "k0p", 0, "xt", 0, x_in[0])
    pick_and_send(1, "k0c", "k0p", 128, [T.off0[:, 2 * d:2 * (d + m)] for i, d, m in runs], [t_off, q_k0], [t_off, q_k0])

    wait("V", ("I", 3), t_low, t_rep32, PA)
    k = done("V", g.vector.tensor_scalar(T.pam[:, :], T.paw[:, :], 511, None, AluOpType.bitwise_and))
    t_fresh = done("V", g.vector.tensor_tensor(T.fresh[:, :], T.base[:, :], T.low[:, :], AluOpType.add))
    t_rep = done("V", g.vector.tensor_copy(T.rep[:, :], T.rep32[:, :]))
    wait("V", k, t_fresh)
    t_pav = done("V", g.vector.tensor_tensor(T.pav[:, :], T.pam[:, :], T.fresh[:, :], AluOpType.min))
    t_ga = spread(0, 1)
    wait("V", SL2)
    for h in range(2):
        t_sd = done("V", g.vector.tensor_copy(T.sd[:, h:24:2], T.slw[:, 8:32:2]))
    q_k = quantise("c1", "p1", 0, "xt", 0, x_in[0])
    t_gb = through("A", 1, turn(T.lin, T.ga, 0, 128, t_ga))
    t_ga = spread(1, 3)
    wait("V", t_pav)
    t_pao = done("V", g.vector.tensor_copy(T.paoff[:, :], T.pav[:, :]))
    q_p = quantise("c1", "p1", 256, "xt", 1, x_in[1])
    t_off = table(1, t_gb)
    made[0] = (q_k,)

    stored = {}
    for t in range(1, 4):
        codes, plane = "c%d" % t, "p%d" % t
        off, pao = [T["off%d" % t][:, 2 * i:2 * (i + m)] for i, d, m in runs], T.paoff[:, 8 * t - 8:8 * t]
        here = [t_off, t_pao, q_p]
        here_c, here_p = here + [made[t - 1][0], arrive(t, False)], here + [made[t - 1][-1], arrive(t, True)]
        pick_and_send(t + 1, codes, plane, 384, off, here_c, here_p)
        made[t] = (pick_codes("c%d" % (t + 1), 0, 128, codes, 384, pao, here_c),
                   gather("A", T["p%d" % (t + 1)][:, 0:128], T[plane][:, 0:384].indirect(pao), here_p))
        if t == 1:
            t_lin = turn(T.lin, T.ga, 128, 384, t_ga)
            t_off = table(2, through("V", 2, t_lin))
            t_gb = through("A", 3, t_lin)
        if t == 2:
            t_off = table(3, t_gb)
        q_p = quantise("c%d" % (t + 1), "p%d" % (t + 1), 256, "xt", t + 1, x_in[t + 1])
        for i in {1: [0], 2: [1, 2], 3: [3, 4]}[t]:
            q_w[i] = quantise("wc", "wp", 128 * i, "wt", i, w_in[i])
        for i in {1: [], 2: [0], 3: [1, 2, 3]}[t]:
            stored[i] = out_block(i)

    halves = [(0, 64, T.paoff[:, 24:28]), (64, 128, T.paoff[:, 28:32])]
    for a, b, pao in halves:
        kc = pick_codes("c5", a, b, "c4", 384, pao, [q_p, made[3][0], arrive(R, False)])
    made[4] = [kc] + [gather(q, T.p5[:, a:b], T.p4[:, 0:384].indirect(pao), [q_p, made[3][1], arrive(R, True)])
                      for q, (a, b, pao) in zip("AV", halves)]
    wait("V", product(4))
    last = done("V", g.vector.tensor_copy(T.ysb[:, 512:640], T.ps[:, 2048:2176]))

    wait("Y", ("lc1", left(1, False)))
    load("Y", "dw34", T.wt[:, xcols(3, 5)], T.w[:, xcols(3, 5)])
    wait("Y", ("lx", sum(left(t, k) for t in range(1, R + 1) for k in (False, True)) - left(1, False)), stored[3])
    load("Y", "dy03", T.y[:, 0:512], T.ysb[:, 0:512])
    wait("Y", last)
    load("Y", "dy4", T.y[:, 512:640], T.ysb[:, 512:640])
    wait("Y", ("dy03", 16), ("dy4", 16))
